import numpy as np
import ml_dtypes


def mxq(x, axis, fmt="e4m3"):
    dtype, down = {"e4m3": (ml_dtypes.float8_e4m3fn, 7), "e5m2": (ml_dtypes.float8_e5m2, 14)}[fmt]
    v = np.moveaxis(np.asarray(x, np.float32).astype(ml_dtypes.bfloat16).astype(np.float64), axis, -1)
    blocks = v.reshape(v.shape[:-1] + (-1, 32))
    amax = np.abs(blocks).max(-1, keepdims=True)
    byte = np.maximum(np.where(amax > 0, np.frexp(amax)[1] - 1 + 127, 0) - down, 1)
    scale = np.exp2(byte - 127.0)
    codes = (blocks / scale).astype(np.float32).astype(dtype).astype(np.float64)
    return np.moveaxis((codes * scale).reshape(v.shape), -1, axis)


WIDE = False


def mx_kscale(k):
    if not WIDE:
        return np.ones(k)
    levels = np.array([10, -10, 5, -5, 0])
    if k % 512:
        return np.exp2(np.random.permutation(np.resize(levels, k // 32))).repeat(32)
    a = np.empty((k // 512, 16))
    for p in range(k // 512):
        a[p, :8] = np.random.permutation(np.resize(levels, 8))
        for g in range(8):
            far = levels[np.abs(levels - a[p, g]) >= 10]
            a[p, g + 8] = far[np.random.randint(len(far))]
    return np.exp2(a.ravel()).repeat(32)


BF16 = ml_dtypes.bfloat16


def bf(x):
    return np.asarray(x, np.float32).astype(BF16)


def f64(x):
    return np.asarray(x).astype(np.float64)


E2M1 = np.array([0.0, 0.5, 1.0, 1.5, 2.0, 3.0, 4.0, 6.0, -0.0, -0.5, -1.0, -1.5, -2.0, -3.0, -4.0, -6.0])


def pack_weight(w, fmt):
    k, n = w.shape
    w = f64(bf(w)).reshape(k // 32, 32, n)
    amax = np.abs(w).max(1)
    if fmt == "e4m3":
        byte = np.frexp(amax)[1] - 1 + 127 - 7
    else:
        mant, ex = np.frexp(amax / 6.0)
        byte = np.where(mant > 0.5, ex, ex - 1) + 127
    byte = np.clip(np.where(amax > 0, byte, 1), 1, 254)
    scaled = (w * np.exp2(127.0 - byte)[:, None, :]).reshape(k, n).astype(np.float32)
    by_word = np.ascontiguousarray(scaled.reshape(k // 512, 128, 4, n).transpose(0, 1, 3, 2))
    if fmt == "e4m3":
        words = by_word.astype(ml_dtypes.float8_e4m3fn).view(np.uint8)
    else:
        c = by_word.astype(ml_dtypes.float4_e2m1fn).view(np.uint8) & 0xF
        words = c[..., 0::2] | (c[..., 1::2] << 4)
    return np.ascontiguousarray(words), np.ascontiguousarray(byte.astype(np.uint8).reshape(k // 512, 16, n))


def unpack_weight(words, scales, fmt):
    g, p, n, _ = words.shape
    if fmt == "e4m3":
        vals = np.ascontiguousarray(words).view(ml_dtypes.float8_e4m3fn).astype(np.float64)
    else:
        nib = np.empty((g, p, n, 4), np.uint8)
        nib[..., 0::2] = words & 0xF
        nib[..., 1::2] = words >> 4
        vals = E2M1[nib]
    vals = vals * np.repeat(np.exp2(scales.astype(np.float64) - 127.0), 8, axis=1)[..., None]
    return vals.transpose(0, 1, 3, 2).reshape(g * 512, n)
def pack4(w):
    words, scales = pack_weight(w, "e2m1")
    return words.reshape(words.shape[0], 128, -1), scales


def unpack4(words, scales):
    return unpack_weight(words.reshape(words.shape[0], 128, -1, 2), scales, "e2m1")


E4M3FN = np.array([(-1.0 if i & 128 else 1.0) * ((1.0 + (i & 7) / 8.0) * 2.0 ** (((i >> 3) & 15) - 7) if i & 120 else (i & 7) * 2.0 ** -9) for i in range(256)])


def e4m3fn_bytes(y):
    return np.clip(np.asarray(y, np.float64), -448.0, 448.0).astype(np.float32).astype(ml_dtypes.float8_e4m3fn).view(np.uint8)


def e4m3fn_values(b):
    return E4M3FN[b]


T, D, E, N, G = 4096, 512, 1024, 2048, 128


def setup_inputs():
    s, t = mx_kscale(T), mx_kscale(E)
    keys = np.random.standard_normal((T, D)) * s[:, None]
    vals = np.random.standard_normal((T, E)) / np.sqrt(T) / s[:, None]
    keys_scale = (np.abs(keys).reshape(T, D // G, G).max(axis=2) / 448.0).astype(np.float32)
    vals_scale = (np.abs(vals).reshape(T, E // G, G).max(axis=2) / 448.0).astype(np.float32)
    w_words, w_scales = pack4(np.random.standard_normal((E, N)) / np.sqrt(E) / t[:, None])
    return {"keys_bytes": e4m3fn_bytes(keys / np.repeat(f64(keys_scale), G, axis=1)),
            "keys_scale": keys_scale,
            "vals_bytes": e4m3fn_bytes(vals / np.repeat(f64(vals_scale), G, axis=1)),
            "vals_scale": vals_scale,
            "prev_state": bf(np.random.standard_normal((D, E))),
            "decay": bf(np.random.uniform(0.5, 0.95, D)),
            "gain": bf((1 + 0.1 * np.random.standard_normal(E)) * t),
            "w_words": w_words, "w_scales": w_scales}


def reference(keys_bytes, keys_scale, vals_bytes, vals_scale, prev_state, decay, gain, w_words, w_scales):
    keys = e4m3fn_values(keys_bytes) * np.repeat(f64(keys_scale), G, axis=1)
    vals = e4m3fn_values(vals_bytes) * np.repeat(f64(vals_scale), G, axis=1)
    kv = mxq(keys, 0, "e4m3").T @ mxq(vals, 0, "e4m3")
    state = f64(decay)[:, None] * f64(prev_state) + kv
    h = state * f64(gain)[None, :]
    y = mxq(h, 1, "e4m3") @ unpack4(w_words, w_scales)
    return state, y

@@ -1,0 +1,336 @@
+from contextlib import ExitStack
+
+import concourse.mybir as mybir
+from concourse.masks import make_identity
+
+T, D, E, N = 4096, 512, 1024, 2048
+FLOPS = 2 * T * D * E + 2 * D * E * N
+
+F32 = mybir.dt.float32
+BF16 = mybir.dt.bfloat16
+I32 = mybir.dt.int32
+U32 = mybir.dt.uint32
+U8 = mybir.dt.uint8
+F8 = mybir.dt.float8_e4m3fn
+FP8X4 = mybir.dt.float8_e4m3fn_x4
+FP4X4 = mybir.dt.float4_e2m1fn_x4
+MULT = mybir.AluOpType.mult
+ADD = mybir.AluOpType.add
+COPY = mybir.ActivationFunctionType.Copy
+
+P = 128
+PASSES = T // 512
+
+
+def tile_fp8_linear_attention_state_d4_kernel(
+    tc, keys_bytes, keys_scale, vals_bytes, vals_scale, prev_state, decay, gain, w_words, w_scales, state_out, y_out
+):
+    nc = tc.nc
+    with ExitStack() as ctx:
+        keep = ctx.enter_context(tc.tile_pool(name="keep", bufs=1))
+        raw = ctx.enter_context(tc.tile_pool(name="raw", bufs=8))
+        stage = ctx.enter_context(tc.tile_pool(name="stage", bufs=3))
+        post = ctx.enter_context(tc.tile_pool(name="post", bufs=2))
+        kvp = ctx.enter_context(tc.psum_pool(name="kvp", bufs=4))
+        pxp = ctx.enter_context(tc.psum_pool(name="pxp", bufs=4))
+        ctx.enter_context(tc.manual_schedule())
+
+        kb_view = keys_bytes.rearrange("(g p t) c -> g p t c", p=P, t=4)
+        vb_view = vals_bytes.rearrange("(g p t) c -> g p t c", p=P, t=4)
+        ks_view = keys_scale.rearrange("(g p t) b -> p g (t b)", p=P, t=4)
+        vs_view = vals_scale.rearrange("(g p t) b -> p g (t b)", p=P, t=4)
+        k_sc0 = keep.tile([P, 16], F32, name="k_sc0")
+        v_sc0 = keep.tile([P, 32], F32, name="v_sc0")
+        k_sc = keep.tile([P, PASSES - 1, 16], F32, name="k_sc")
+        v_sc = keep.tile([P, PASSES - 1, 32], F32, name="v_sc")
+        kbytes = []
+        vbytes = []
+        nc.sync.dma_start(out=k_sc0[:], in_=ks_view[:, 0, :])
+        for g in range(PASSES):
+            kb = raw.tile([P, 4, D], U8, name="kb")
+            nc.sync.dma_start(out=kb[:], in_=kb_view[g])
+            if g == 0:
+                nc.sync.dma_start(out=v_sc0[:], in_=vs_view[:, 0, :])
+            vb = raw.tile([P, 4, E], U8, name="vb")
+            nc.sync.dma_start(out=vb[:], in_=vb_view[g])
+            if g == 0:
+                nc.sync.dma_start(out=k_sc[:], in_=ks_view[:, 1:, :])
+                nc.sync.dma_start(out=v_sc[:], in_=vs_view[:, 1:, :])
+            kbytes.append(kb)
+            vbytes.append(vb)
+        dec_rows = keep.tile([4, P], BF16, name="dec_rows")
+        nc.sync.dma_start(out=dec_rows[:], in_=decay.rearrange("(d p) -> d p", p=P))
+        prev = keep.tile([P, 4, E], BF16, name="prev")
+        nc.sync.dma_start(out=prev[:], in_=prev_state.rearrange("(d p) e -> p d e", p=P))
+        gain_b = keep.tile([P, E], BF16, name="gain_b")
+        nc.sync.dma_start(out=gain_b[:], in_=gain.partition_broadcast(P))
+
+        wsc = keep.tile([P, 2, N], U8, name="wsc", align_bytes=64)
+        ident = keep.tile([P, P], F32, name="ident")
+        dec_sq = keep.tile([P, P], F32, name="dec_sq")
+        make_identity(nc, ident[:])
+        nc.gpsimd.memset(dec_sq[:], 0.0)
+        nc.gpsimd.memset(wsc[:].rearrange("p g n -> p (g n)").bitcast(I32), 0)
+        for q in range(4):
+            nc.sync.dma_start(
+                out=wsc[32 * q : 32 * q + 4].bitcast(I32),
+                in_=w_scales[:, 4 * q : 4 * q + 4, :].rearrange("g q n -> q g n").bitcast(I32),
+            )
+        ww = keep.tile([P, 2, 2 * N], U8, name="ww", align_bytes=64)
+        for g in range(2):
+            nc.sync.dma_start(out=ww[:, g, :].bitcast(I32), in_=w_words[g].bitcast(I32))
+
+        def kscale(g, i):
+            return k_sc0[:, i : i + 1] if g == 0 else k_sc[:, g - 1, i : i + 1]
+
+        def vscale(g, i):
+            return v_sc0[:, i : i + 1] if g == 0 else v_sc[:, g - 1, i : i + 1]
+
+        vc = keep.tile([P, PASSES, E], U32, name="vc", align_bytes=64)
+        vpl = keep.tile([P, PASSES, E], U8, name="vpl", align_bytes=64)
+        ka = keep.tile([P, PASSES, 256], U32, name="ka", align_bytes=64)
+        kapl = keep.tile([P, PASSES, 256], U8, name="kapl", align_bytes=64)
+        kbc = keep.tile([P, 2, PASSES, P], U32, name="kbc", align_bytes=64)
+        kbpl = keep.tile([P, 2, PASSES, P], U8, name="kbpl", align_bytes=64)
+
+        units = []
+        for g in range(PASSES):
+            units.append(("k", g, 0))
+            units.append(("v", g, 0))
+            units.append(("v", g, 1))
+        for dd in range(2):
+            for hf in range(2):
+                units.append(("b", dd, hf))
+        n_units = len(units)
+
+        def jobs(u):
+            kind, a, b = u
+            out = []
+            if kind == "k":
+                for t in range(4):
+                    for blk in range(2):
+                        out.append((kbytes[a][:, t, blk * P : blk * P + P], t, blk, kscale(a, 4 * t + blk)))
+            elif kind == "v":
+                for t in range(4):
+                    for blk in range(4):
+                        c = b * 4 + blk
+                        out.append((vbytes[a][:, t, c * P : c * P + P], t, blk, vscale(a, 8 * t + c)))
+            else:
+                for t in range(4):
+                    for i in range(4):
+                        g = 4 * b + i
+                        blk = 2 + a
+                        out.append((kbytes[g][:, t, blk * P : blk * P + P], t, i, kscale(g, 4 * t + blk)))
+            return out
+
+        wide = {}
+        grp = {}
+
+        def widen(i, n_vec):
+            js = jobs(units[i])
+            w = stage.tile([P, 4, 512], BF16, name="w", bufs=4, align_bytes=64)
+            wide[i] = w
+            for k, (src, t, blk, sc) in enumerate(js):
+                dst = w[:, t, blk * P : blk * P + P]
+                if k < n_vec:
+                    nc.vector.tensor_scalar(out=dst, in0=src.bitcast(F8), scalar1=sc, scalar2=None, op0=MULT)
+                else:
+                    nc.scalar.activation(out=dst, in_=src.bitcast(F8), func=COPY, scale=sc)
+
+        def interleave(i):
+            cols = 256 if units[i][0] == "k" else 512
+            gt = stage.tile([P, 512, 4], BF16, name="gt", bufs=3, align_bytes=64)
+            grp[i] = gt
+            nc.vector.tensor_copy(
+                out=gt[:, :cols, :].rearrange("p (c i) t -> p c t i", i=4),
+                in_=wide[i][:, :, :cols].rearrange("p t (c i) -> p c t i", i=4),
+            )
+
+        def quantise(i):
+            kind, a, b = units[i]
+            cols = 256 if kind == "k" else 512
+            if kind == "k":
+                co, pl = ka[:, a, :], kapl[:, a, :]
+            elif kind == "v":
+                co, pl = vc[:, a, b * 512 : b * 512 + 512], vpl[:, a, b * 512 : b * 512 + 512]
+            else:
+                co = kbc[:, a, 4 * b : 4 * b + 4, :].rearrange("p g c -> p (g c)")
+                pl = kbpl[:, a, 4 * b : 4 * b + 4, :].rearrange("p g c -> p (g c)")
+            nc.vector.quantize_mx(
+                out=co.bitcast(FP8X4), scales=pl, in_=grp[i][:, :cols, :].rearrange("p c t -> p (c t)")
+            )
+
+        kv = {}
+
+        def mm(dt, eh, g):
+            if g == 0:
+                acc = kvp.tile([P, 512], F32, name="acc")
+                kv[dt, eh] = acc
+            if dt < 2:
+                lc, lp = ka[:, g, dt * P : dt * P + P], kapl[:, g, dt * P : dt * P + P]
+            else:
+                lc, lp = kbc[:, dt - 2, g, :], kbpl[:, dt - 2, g, :]
+            nc.tensor.matmul_mx(
+                out=kv[dt, eh][:],
+                lhsT=lc.bitcast(FP8X4),
+                lhsT_scale=lp,
+                rhs=vc[:, g, eh * 512 : eh * 512 + 512].bitcast(FP8X4),
+                rhs_scale=vpl[:, g, eh * 512 : eh * 512 + 512],
+                start=(g == 0),
+                stop=(g == PASSES - 1),
+            )
+
+        def multiply(i):
+            kind, a, b = units[i]
+            if kind == "v":
+                mm(0, b, a)
+                mm(1, b, a)
+            elif kind == "b":
+                for eh in range(2):
+                    for g in range(4 * b, 4 * b + 4):
+                        mm(2 + a, eh, g)
+
+        dec_c = keep.tile([P, 4], F32, name="dec_c")
+
+        def decay_columns():
+            nc.vector.tensor_copy(out=dec_sq[0:4, :], in_=dec_rows[:])
+            dt_ps = pxp.tile([P, P], F32, name="px")
+            nc.tensor.transpose(dt_ps[:], dec_sq[:], ident[:])
+            nc.vector.tensor_copy(out=dec_c[:], in_=dt_ps[:, 0:4])
+
+        st, hb, xt, hg, hc, hp, ys, yo = {}, {}, {}, {}, {}, {}, {}, {}
+
+        def state(dt, eh):
+            if eh == 0:
+                s_t = post.tile([P, E], F32, name="s_t", bufs=3)
+                st[dt] = s_t
+            sl = slice(eh * 512, eh * 512 + 512)
+            nc.vector.scalar_tensor_tensor(
+                out=st[dt][:, sl], in0=prev[:, dt, sl], scalar=dec_c[:, dt : dt + 1], in1=kv[dt, eh][:], op0=MULT, op1=ADD
+            )
+            if eh == 1:
+                nc.sync.dma_start(out=state_out[dt * P : dt * P + P, :], in_=st[dt][:])
+
+        def gained(dt):
+            h_t = post.tile([P, E], BF16, name="h_t")
+            hb[dt] = h_t
+            nc.vector.tensor_tensor(out=h_t[:], in0=st[dt][:], in1=gain_b[:], op=MULT)
+
+        def turn(dt):
+            x_t = pxp.tile([P, 2, 2, P], F32, name="px")
+            xt[dt] = x_t
+            words = hb[dt][:].bitcast(F32)
+            for g in range(2):
+                for u in range(2):
+                    nc.tensor.transpose(x_t[:, g, u, :], words[:, 256 * g + u : 256 * (g + 1) : 2], ident[:])
+
+        def turned(dt):
+            g_t = post.tile([P, 2, P, 4], BF16, name="g_t", align_bytes=64)
+            hg[dt] = g_t
+            nc.scalar.copy(
+                out=g_t[:].rearrange("p g r t -> p (g r t)").bitcast(F32).rearrange("p (g r u) -> p g r u", g=2, u=2),
+                in_=xt[dt][:].rearrange("p g u r -> p g r u"),
+            )
+
+        def quantise_h(dt):
+            c_t = post.tile([P, 256], U32, name="c_t", align_bytes=64)
+            p_t = post.tile([P, 256], U8, name="p_t", align_bytes=64)
+            hc[dt], hp[dt] = c_t, p_t
+            nc.vector.quantize_mx(
+                out=c_t[:].bitcast(FP8X4), scales=p_t[:], in_=hg[dt][:].rearrange("p g r t -> p (g r t)")
+            )
+
+        def project(dt, n):
+            y_p = pxp.tile([P, 512], F32, name="px")
+            ys[dt, n] = y_p
+            for g in range(2):
+                nc.tensor.matmul_mx(
+                    out=y_p[:],
+                    lhsT=hc[dt][:, g * P : g * P + P].bitcast(FP8X4),
+                    lhsT_scale=hp[dt][:, g * P : g * P + P],
+                    rhs=ww[:, g, n * 1024 : n * 1024 + 1024].bitcast(FP4X4),
+                    rhs_scale=wsc[:, g, n * 512 : n * 512 + 512],
+                    start=(g == 0),
+                    stop=(g == 1),
+                )
+
+        def leave(dt, n, eng):
+            if n == 0:
+                y_t = post.tile([P, N], F32, name="y_t", bufs=3)
+                yo[dt] = y_t
+            dst = yo[dt][:, n * 512 : n * 512 + 512]
+            if eng == "s":
+                nc.scalar.copy(out=dst, in_=ys[dt, n][:])
+            else:
+                nc.vector.tensor_copy(out=dst, in_=ys[dt, n][:])
+            if n % 2 == 1:
+                sl = slice((n - 1) * 512, (n + 1) * 512)
+                nc.sync.dma_start(out=y_out[dt * P : dt * P + P, sl], in_=yo[dt][:, sl])
+
+        def n_vec(i):
+            if i == 0:
+                return 5
+            kind = units[i][0]
+            return {"k": 1, "v": 3, "b": 0}[kind]
+
+        last = n_units - 1
+        for i in range(n_units):
+            widen(i, n_vec(i))
+            if i >= 1:
+                interleave(i - 1)
+            if i == 6:
+                decay_columns()
+            if i == 26:
+                state(0, 0)
+                state(0, 1)
+            if i == 27:
+                gained(0)
+                turn(0)
+                turned(0)
+                state(1, 0)
+                state(1, 1)
+            if i >= 2:
+                quantise(i - 2)
+                multiply(i - 2)
+        interleave(27)
+        quantise_h(0)
+        gained(1)
+        project(0, 0)
+        project(0, 1)
+        turn(1)
+        leave(0, 0, "s")
+        leave(0, 1, "s")
+        state(2, 0)
+        state(2, 1)
+        quantise(26)
+        project(0, 2)
+        project(0, 3)
+        turned(1)
+        leave(0, 2, "s")
+        leave(0, 3, "s")
+        multiply(26)
+        gained(2)
+        quantise(27)
+        quantise_h(1)
+        multiply(27)
+        turn(2)
+        turned(2)
+        for n in range(4):
+            project(1, n)
+            leave(1, n, "s")
+        state(3, 0)
+        state(3, 1)
+        quantise_h(2)
+        gained(3)
+        for n in range(2):
+            project(2, n)
+            leave(2, n, "s")
+        turn(3)
+        turned(3)
+        for n in range(2, 4):
+            project(2, n)
+            leave(2, n, "v")
+        quantise_h(3)
+        for n in range(4):
+            project(3, n)
+            leave(3, n, "sv"[n % 2])

@@ -20,6 +20,17 @@ COPY = mybir.ActivationFunctionType.Copy
 
 P = 128
 PASSES = T // 512
+HALF = 512
+LEAD = 2
+QLAG = 3
+LEAVE = ("ssss", "ssss", "ssss", "vsvs")
+TURNED = "ssss"
+NV_PE, NV_VE, NV_FIRST = 13, 7, 4
+N_LATE, NV_LATE = 16, 9
+PE_COLS = {(g, h): 512 for g in range(4) for h in range(2)}
+PE_COLS[4, 0] = 512
+PE_COLS[4, 1] = 256
+B_AFTER = {3: [(0, 0)], 5: [(0, 1)]}
 
 
 def tile_fp8_linear_attention_state_d4_kernel(
@@ -31,35 +42,38 @@ def tile_fp8_linear_attention_state_d4_kernel(
         raw = ctx.enter_context(tc.tile_pool(name="raw", bufs=8))
         stage = ctx.enter_context(tc.tile_pool(name="stage", bufs=3))
         post = ctx.enter_context(tc.tile_pool(name="post", bufs=2))
-        kvp = ctx.enter_context(tc.psum_pool(name="kvp", bufs=4))
-        pxp = ctx.enter_context(tc.psum_pool(name="pxp", bufs=4))
+        psum = ctx.enter_context(tc.psum_pool(name="psum", bufs=1))
         ctx.enter_context(tc.manual_schedule())
 
         kb_view = keys_bytes.rearrange("(g p t) c -> g p t c", p=P, t=4)
         vb_view = vals_bytes.rearrange("(g p t) c -> g p t c", p=P, t=4)
         ks_view = keys_scale.rearrange("(g p t) b -> p g (t b)", p=P, t=4)
         vs_view = vals_scale.rearrange("(g p t) b -> p g (t b)", p=P, t=4)
-        k_sc0 = keep.tile([P, 16], F32, name="k_sc0")
-        v_sc0 = keep.tile([P, 32], F32, name="v_sc0")
-        k_sc = keep.tile([P, PASSES - 1, 16], F32, name="k_sc")
-        v_sc = keep.tile([P, PASSES - 1, 32], F32, name="v_sc")
-        kbytes = []
-        vbytes = []
-        nc.sync.dma_start(out=k_sc0[:], in_=ks_view[:, 0, :])
+        kbytes, vbytes, kscales, vscales = [], [], {}, {}
+
+        def load_scales(first, last):
+            k_sc = keep.tile([P, last - first, 16], F32, name="k_sc%d" % first)
+            v_sc = keep.tile([P, last - first, 32], F32, name="v_sc%d" % first)
+            nc.sync.dma_start(out=k_sc[:], in_=ks_view[:, first:last, :])
+            nc.sync.dma_start(out=v_sc[:], in_=vs_view[:, first:last, :])
+            for g in range(first, last):
+                kscales[g] = k_sc[:, g - first, :]
+                vscales[g] = v_sc[:, g - first, :]
+
+        dec_rows = keep.tile([4, P], BF16, name="dec_rows")
         for g in range(PASSES):
+            if g < 2:
+                load_scales(g, g + 1)
             kb = raw.tile([P, 4, D], U8, name="kb")
             nc.sync.dma_start(out=kb[:], in_=kb_view[g])
-            if g == 0:
-                nc.sync.dma_start(out=v_sc0[:], in_=vs_view[:, 0, :])
             vb = raw.tile([P, 4, E], U8, name="vb")
             nc.sync.dma_start(out=vb[:], in_=vb_view[g])
             if g == 0:
-                nc.sync.dma_start(out=k_sc[:], in_=ks_view[:, 1:, :])
-                nc.sync.dma_start(out=v_sc[:], in_=vs_view[:, 1:, :])
+                nc.sync.dma_start(out=dec_rows[:], in_=decay.rearrange("(d p) -> d p", p=P))
+            if g == 1:
+                load_scales(2, PASSES)
             kbytes.append(kb)
             vbytes.append(vb)
-        dec_rows = keep.tile([4, P], BF16, name="dec_rows")
-        nc.sync.dma_start(out=dec_rows[:], in_=decay.rearrange("(d p) -> d p", p=P))
         prev = keep.tile([P, 4, E], BF16, name="prev")
         nc.sync.dma_start(out=prev[:], in_=prev_state.rearrange("(d p) e -> p d e", p=P))
         gain_b = keep.tile([P, E], BF16, name="gain_b")
@@ -67,7 +81,9 @@ def tile_fp8_linear_attention_state_d4_kernel(
 
         wsc = keep.tile([P, 2, N], U8, name="wsc", align_bytes=64)
         ident = keep.tile([P, P], F32, name="ident")
+        ident_b = keep.tile([P, P], BF16, name="ident_b")
         dec_sq = keep.tile([P, P], F32, name="dec_sq")
+        make_identity(nc, ident_b[:])
         make_identity(nc, ident[:])
         nc.gpsimd.memset(dec_sq[:], 0.0)
         nc.gpsimd.memset(wsc[:].rearrange("p g n -> p (g n)").bitcast(I32), 0)
@@ -80,123 +96,146 @@ def tile_fp8_linear_attention_state_d4_kernel(
         for g in range(2):
             nc.sync.dma_start(out=ww[:, g, :].bitcast(I32), in_=w_words[g].bitcast(I32))
 
-        def kscale(g, i):
-            return k_sc0[:, i : i + 1] if g == 0 else k_sc[:, g - 1, i : i + 1]
-
-        def vscale(g, i):
-            return v_sc0[:, i : i + 1] if g == 0 else v_sc[:, g - 1, i : i + 1]
-
         vc = keep.tile([P, PASSES, E], U32, name="vc", align_bytes=64)
         vpl = keep.tile([P, PASSES, E], U8, name="vpl", align_bytes=64)
-        ka = keep.tile([P, PASSES, 256], U32, name="ka", align_bytes=64)
-        kapl = keep.tile([P, PASSES, 256], U8, name="kapl", align_bytes=64)
-        kbc = keep.tile([P, 2, PASSES, P], U32, name="kbc", align_bytes=64)
-        kbpl = keep.tile([P, 2, PASSES, P], U8, name="kbpl", align_bytes=64)
+        ka = keep.tile([P, PASSES, D], U32, name="ka", align_bytes=64)
+        kapl = keep.tile([P, PASSES, D], U8, name="kapl", align_bytes=64)
 
         units = []
         for g in range(PASSES):
-            units.append(("k", g, 0))
-            units.append(("v", g, 0))
-            units.append(("v", g, 1))
-        for dd in range(2):
-            for hf in range(2):
-                units.append(("b", dd, hf))
+            units += [("k", g, 0), ("v", g, 0), ("v", g, 1)]
         n_units = len(units)
+
+        def pe_cols(i):
+            kind, a, b = units[i]
+            return PE_COLS.get((a, b), 0) if kind == "v" else 0
+
+        def n_vec(i):
+            if i == 0:
+                return NV_FIRST
+            if pe_cols(i):
+                return NV_PE
+            return NV_VE if i < N_LATE else max(0, NV_LATE - (i - N_LATE))
 
         def jobs(u):
             kind, a, b = u
             out = []
             if kind == "k":
-                for t in range(4):
-                    for blk in range(2):
-                        out.append((kbytes[a][:, t, blk * P : blk * P + P], t, blk, kscale(a, 4 * t + blk)))
-            elif kind == "v":
-                for t in range(4):
-                    for blk in range(4):
-                        c = b * 4 + blk
-                        out.append((vbytes[a][:, t, c * P : c * P + P], t, blk, vscale(a, 8 * t + c)))
+                for blk in range(4):
+                    for t in range(4):
+                        out.append((kbytes[a][:, t, blk * P : blk * P + P], t, blk, kscales[a][:, 4 * t + blk : 4 * t + blk + 1]))
             else:
-                for t in range(4):
-                    for i in range(4):
-                        g = 4 * b + i
-                        blk = 2 + a
-                        out.append((kbytes[g][:, t, blk * P : blk * P + P], t, i, kscale(g, 4 * t + blk)))
+                for blk in range(4):
+                    for t in range(4):
+                        c = b * 4 + blk
+                        out.append((vbytes[a][:, t, c * P : c * P + P], t, blk, vscales[a][:, 8 * t + c : 8 * t + c + 1]))
             return out
 
-        wide = {}
-        grp = {}
+        banks = {"next": 0, "ring": [6, 7]}
 
-        def widen(i, n_vec):
+        def bank(b, shape, dt):
+            return psum.tile(shape, dt, name="bank%d" % b)
+
+        def ring(shape, dt):
+            b = banks["ring"][banks["next"] % len(banks["ring"])]
+            banks["next"] += 1
+            return bank(b, shape, dt)
+
+        wide, grp, lain = {}, {}, {}
+
+        def widen(i):
             js = jobs(units[i])
-            w = stage.tile([P, 4, 512], BF16, name="w", bufs=4, align_bytes=64)
+            w = stage.tile([P, 4, HALF], BF16, name="w", bufs=6, align_bytes=64)
             wide[i] = w
             for k, (src, t, blk, sc) in enumerate(js):
                 dst = w[:, t, blk * P : blk * P + P]
-                if k < n_vec:
+                if k < n_vec(i):
                     nc.vector.tensor_scalar(out=dst, in0=src.bitcast(F8), scalar1=sc, scalar2=None, op0=MULT)
                 else:
                     nc.scalar.activation(out=dst, in_=src.bitcast(F8), func=COPY, scale=sc)
 
         def interleave(i):
-            cols = 256 if units[i][0] == "k" else 512
-            gt = stage.tile([P, 512, 4], BF16, name="gt", bufs=3, align_bytes=64)
+            gt = stage.tile([P, HALF, 4], BF16, name="gt", bufs=6, align_bytes=64)
             grp[i] = gt
-            nc.vector.tensor_copy(
-                out=gt[:, :cols, :].rearrange("p (c i) t -> p c t i", i=4),
-                in_=wide[i][:, :, :cols].rearrange("p t (c i) -> p c t i", i=4),
-            )
+            by_pe = pe_cols(i)
+            for c0 in range(0, by_pe, 256):
+                b_t = ring([P, 256, 4], BF16)
+                for c1 in range(0, 256, P):
+                    nc.tensor.matmul(
+                        out=b_t[:, c1 : c1 + P, :].rearrange("p c t -> p (c t)"),
+                        lhsT=ident_b[:],
+                        rhs=wide[i][:, :, c0 + c1 : c0 + c1 + P].rearrange("p t c -> p c t"),
+                        start=True,
+                        stop=True,
+                    )
+                nc.scalar.copy(out=gt[:, c0 : c0 + 256, :], in_=b_t[:])
+            if by_pe < HALF:
+                nc.vector.tensor_copy(
+                    out=gt[:, by_pe:, :].rearrange("p (c i) t -> p c t i", i=4),
+                    in_=wide[i][:, :, by_pe:].rearrange("p t (c i) -> p c t i", i=4),
+                )
 
         def quantise(i):
             kind, a, b = units[i]
-            cols = 256 if kind == "k" else 512
             if kind == "k":
                 co, pl = ka[:, a, :], kapl[:, a, :]
-            elif kind == "v":
-                co, pl = vc[:, a, b * 512 : b * 512 + 512], vpl[:, a, b * 512 : b * 512 + 512]
             else:
-                co = kbc[:, a, 4 * b : 4 * b + 4, :].rearrange("p g c -> p (g c)")
-                pl = kbpl[:, a, 4 * b : 4 * b + 4, :].rearrange("p g c -> p (g c)")
-            nc.vector.quantize_mx(
-                out=co.bitcast(FP8X4), scales=pl, in_=grp[i][:, :cols, :].rearrange("p c t -> p (c t)")
-            )
+                co, pl = vc[:, a, b * HALF : b * HALF + HALF], vpl[:, a, b * HALF : b * HALF + HALF]
+            nc.vector.quantize_mx(out=co.bitcast(FP8X4), scales=pl, in_=grp[i][:].rearrange("p c t -> p (c t)"))
 
         kv = {}
+        KV_BANK = {(dt, eh): 2 * dt + eh for dt in range(4) for eh in range(2)}
 
         def mm(dt, eh, g):
             if g == 0:
-                acc = kvp.tile([P, 512], F32, name="acc")
+                acc = bank(KV_BANK[dt, eh], [P, HALF], F32)
                 kv[dt, eh] = acc
-            if dt < 2:
-                lc, lp = ka[:, g, dt * P : dt * P + P], kapl[:, g, dt * P : dt * P + P]
-            else:
-                lc, lp = kbc[:, dt - 2, g, :], kbpl[:, dt - 2, g, :]
+            lc, lp = ka[:, g, dt * P : dt * P + P], kapl[:, g, dt * P : dt * P + P]
             nc.tensor.matmul_mx(
                 out=kv[dt, eh][:],
                 lhsT=lc.bitcast(FP8X4),
                 lhsT_scale=lp,
-                rhs=vc[:, g, eh * 512 : eh * 512 + 512].bitcast(FP8X4),
-                rhs_scale=vpl[:, g, eh * 512 : eh * 512 + 512],
+                rhs=vc[:, g, eh * HALF : eh * HALF + HALF].bitcast(FP8X4),
+                rhs_scale=vpl[:, g, eh * HALF : eh * HALF + HALF],
                 start=(g == 0),
                 stop=(g == PASSES - 1),
             )
 
+        ready = set()
+        issued = set()
+        allowed = {0, 1, 2}
+
         def multiply(i):
             kind, a, b = units[i]
             if kind == "v":
-                mm(0, b, a)
-                mm(1, b, a)
-            elif kind == "b":
+                ready.add(("v", b, a))
+            else:
+                ready.update([(dt, a) for dt in range(4)])
+            issue()
+
+        def issue():
+            for dt in sorted(allowed):
                 for eh in range(2):
-                    for g in range(4 * b, 4 * b + 4):
-                        mm(2 + a, eh, g)
+                    for g in range(PASSES):
+                        key = (dt, eh, g)
+                        if key in issued:
+                            continue
+                        if (dt, g) in ready and ("v", eh, g) in ready:
+                            mm(dt, eh, g)
+                            issued.add(key)
+                        else:
+                            break
 
         dec_c = keep.tile([P, 4], F32, name="dec_c")
 
-        def decay_columns():
-            nc.vector.tensor_copy(out=dec_sq[0:4, :], in_=dec_rows[:])
-            dt_ps = pxp.tile([P, P], F32, name="px")
+        def decay_square():
+            nc.scalar.copy(out=dec_sq[0:4, :], in_=dec_rows[:])
+            dt_ps = bank(0, [P, P], F32)
             nc.tensor.transpose(dt_ps[:], dec_sq[:], ident[:])
-            nc.vector.tensor_copy(out=dec_c[:], in_=dt_ps[:, 0:4])
+            return dt_ps
+
+        def decay_columns(dt_ps):
+            nc.scalar.copy(out=dec_c[:], in_=dt_ps[:, 0:4])
 
         st, hb, xt, hg, hc, hp, ys, yo = {}, {}, {}, {}, {}, {}, {}, {}
 
@@ -204,133 +243,120 @@ def tile_fp8_linear_attention_state_d4_kernel(
             if eh == 0:
                 s_t = post.tile([P, E], F32, name="s_t", bufs=3)
                 st[dt] = s_t
-            sl = slice(eh * 512, eh * 512 + 512)
+            sl = slice(eh * HALF, eh * HALF + HALF)
             nc.vector.scalar_tensor_tensor(
                 out=st[dt][:, sl], in0=prev[:, dt, sl], scalar=dec_c[:, dt : dt + 1], in1=kv[dt, eh][:], op0=MULT, op1=ADD
             )
             if eh == 1:
                 nc.sync.dma_start(out=state_out[dt * P : dt * P + P, :], in_=st[dt][:])
 
-        def gained(dt):
-            h_t = post.tile([P, E], BF16, name="h_t")
-            hb[dt] = h_t
-            nc.vector.tensor_tensor(out=h_t[:], in0=st[dt][:], in1=gain_b[:], op=MULT)
+        def gained(dt, eh):
+            if eh == 0:
+                h_t = post.tile([P, E], BF16, name="h_t")
+                hb[dt] = h_t
+            sl = slice(eh * HALF, eh * HALF + HALF)
+            nc.vector.tensor_tensor(out=hb[dt][:, sl], in0=st[dt][:, sl], in1=gain_b[:, sl], op=MULT)
 
-        def turn(dt):
-            x_t = pxp.tile([P, 2, 2, P], F32, name="px")
-            xt[dt] = x_t
+        def turn(dt, g):
+            x_t = ring([P, 2, P], F32)
+            xt[dt, g] = x_t
             words = hb[dt][:].bitcast(F32)
-            for g in range(2):
-                for u in range(2):
-                    nc.tensor.transpose(x_t[:, g, u, :], words[:, 256 * g + u : 256 * (g + 1) : 2], ident[:])
+            for u in range(2):
+                nc.tensor.transpose(x_t[:, u, :], words[:, 256 * g + u : 256 * (g + 1) : 2], ident[:])
 
-        def turned(dt):
-            g_t = post.tile([P, 2, P, 4], BF16, name="g_t", align_bytes=64)
-            hg[dt] = g_t
-            nc.scalar.copy(
-                out=g_t[:].rearrange("p g r t -> p (g r t)").bitcast(F32).rearrange("p (g r u) -> p g r u", g=2, u=2),
-                in_=xt[dt][:].rearrange("p g u r -> p g r u"),
-            )
+        def turned(dt, g, eng="s"):
+            g_t = post.tile([P, P, 4], BF16, name="g_t", bufs=4, align_bytes=64)
+            hg[dt, g] = g_t
+            dst = g_t[:].rearrange("p r t -> p (r t)").bitcast(F32).rearrange("p (r u) -> p r u", u=2)
+            src = xt[dt, g][:].rearrange("p u r -> p r u")
+            if eng == "s":
+                nc.scalar.copy(out=dst, in_=src)
+            else:
+                nc.vector.tensor_copy(out=dst, in_=src)
 
-        def quantise_h(dt):
-            c_t = post.tile([P, 256], U32, name="c_t", align_bytes=64)
-            p_t = post.tile([P, 256], U8, name="p_t", align_bytes=64)
-            hc[dt], hp[dt] = c_t, p_t
+        def quantise_h(dt, g):
+            c_t = post.tile([P, P], U32, name="c_t", bufs=4, align_bytes=64)
+            p_t = post.tile([P, P], U8, name="p_t", bufs=4, align_bytes=64)
+            hc[dt, g], hp[dt, g] = c_t, p_t
             nc.vector.quantize_mx(
-                out=c_t[:].bitcast(FP8X4), scales=p_t[:], in_=hg[dt][:].rearrange("p g r t -> p (g r t)")
+                out=c_t[:].bitcast(FP8X4), scales=p_t[:], in_=hg[dt, g][:].rearrange("p r t -> p (r t)")
             )
 
-        def project(dt, n):
-            y_p = pxp.tile([P, 512], F32, name="px")
-            ys[dt, n] = y_p
-            for g in range(2):
-                nc.tensor.matmul_mx(
-                    out=y_p[:],
-                    lhsT=hc[dt][:, g * P : g * P + P].bitcast(FP8X4),
-                    lhsT_scale=hp[dt][:, g * P : g * P + P],
-                    rhs=ww[:, g, n * 1024 : n * 1024 + 1024].bitcast(FP4X4),
-                    rhs_scale=wsc[:, g, n * 512 : n * 512 + 512],
-                    start=(g == 0),
-                    stop=(g == 1),
-                )
+        def project(dt, n, g):
+            if g == 0:
+                y_p = ring([P, HALF], F32)
+                ys[dt, n] = y_p
+            nc.tensor.matmul_mx(
+                out=ys[dt, n][:],
+                lhsT=hc[dt, g][:].bitcast(FP8X4),
+                lhsT_scale=hp[dt, g][:],
+                rhs=ww[:, g, n * 1024 : n * 1024 + 1024].bitcast(FP4X4),
+                rhs_scale=wsc[:, g, n * HALF : n * HALF + HALF],
+                start=(g == 0),
+                stop=(g == 1),
+            )
 
         def leave(dt, n, eng):
             if n == 0:
                 y_t = post.tile([P, N], F32, name="y_t", bufs=3)
                 yo[dt] = y_t
-            dst = yo[dt][:, n * 512 : n * 512 + 512]
+            dst = yo[dt][:, n * HALF : n * HALF + HALF]
             if eng == "s":
                 nc.scalar.copy(out=dst, in_=ys[dt, n][:])
             else:
                 nc.vector.tensor_copy(out=dst, in_=ys[dt, n][:])
             if n % 2 == 1:
-                sl = slice((n - 1) * 512, (n + 1) * 512)
+                sl = slice((n - 1) * HALF, (n + 1) * HALF)
                 nc.sync.dma_start(out=y_out[dt * P : dt * P + P, sl], in_=yo[dt][:, sl])
 
-        def n_vec(i):
-            if i == 0:
-                return 5
-            kind = units[i][0]
-            return {"k": 1, "v": 3, "b": 0}[kind]
+        pe_last = max(i for i in range(n_units) if pe_cols(i))
+        for i in range(n_units + LEAD + QLAG):
+            if i < n_units:
+                widen(i)
+            if i == 3:
+                turned_decay = decay_square()
+            if i == 4:
+                decay_columns(turned_decay)
+            j = i - LEAD
+            if 0 <= j < n_units:
+                interleave(j)
+                if j == pe_last:
+                    allowed.add(3)
+            j = i - LEAD - QLAG
+            if 0 <= j:
+                quantise(j)
+                multiply(j)
 
-        last = n_units - 1
-        for i in range(n_units):
-            widen(i, n_vec(i))
-            if i >= 1:
-                interleave(i - 1)
-            if i == 6:
-                decay_columns()
-            if i == 26:
-                state(0, 0)
-                state(0, 1)
-            if i == 27:
-                gained(0)
-                turn(0)
-                turned(0)
-                state(1, 0)
-                state(1, 1)
-            if i >= 2:
-                quantise(i - 2)
-                multiply(i - 2)
-        interleave(27)
-        quantise_h(0)
-        gained(1)
-        project(0, 0)
-        project(0, 1)
-        turn(1)
-        leave(0, 0, "s")
-        leave(0, 1, "s")
-        state(2, 0)
-        state(2, 1)
-        quantise(26)
-        project(0, 2)
-        project(0, 3)
-        turned(1)
-        leave(0, 2, "s")
-        leave(0, 3, "s")
-        multiply(26)
-        gained(2)
-        quantise(27)
-        quantise_h(1)
-        multiply(27)
-        turn(2)
-        turned(2)
-        for n in range(4):
-            project(1, n)
-            leave(1, n, "s")
-        state(3, 0)
-        state(3, 1)
-        quantise_h(2)
-        gained(3)
-        for n in range(2):
-            project(2, n)
-            leave(2, n, "s")
-        turn(3)
-        turned(3)
-        for n in range(2, 4):
-            project(2, n)
-            leave(2, n, "v")
-        quantise_h(3)
-        for n in range(4):
-            project(3, n)
-            leave(3, n, "sv"[n % 2])
+        def turns(dt):
+            turn(dt, 0)
+            turn(dt, 1)
+            turned(dt, 0, TURNED[dt])
+            turned(dt, 1, TURNED[dt])
+
+        def projects(dt, first):
+            for n in (first, first + 1):
+                project(dt, n, 0)
+                project(dt, n, 1)
+                leave(dt, n, LEAVE[dt][n])
+
+        banks["ring"] = [0, 2, 1, 3, 4, 5, 6, 7]
+        banks["next"] = 0
+        state(0, 0)
+        state(1, 0)
+        state(0, 1)
+        gained(0, 0)
+        gained(0, 1)
+        turns(0)
+        state(1, 1)
+        for dt in range(4):
+            quantise_h(dt, 0)
+            quantise_h(dt, 1)
+            projects(dt, 0)
+            if dt < 3:
+                gained(dt + 1, 0)
+                gained(dt + 1, 1)
+                turns(dt + 1)
+            if dt < 2:
+                state(dt + 2, 0)
+                state(dt + 2, 1)
+            projects(dt, 2)

@@ -25,11 +25,9 @@ LEAD = 2
 QLAG = 3
 LEAVE = ("ssss", "ssss", "ssss", "vsvs")
 TURNED = "ssss"
-NV_PE, NV_VE, NV_FIRST = 13, 7, 4
-N_LATE, NV_LATE = 16, 9
-PE_COLS = {(g, h): 512 for g in range(4) for h in range(2)}
-PE_COLS[4, 0] = 512
-PE_COLS[4, 1] = 256
+NV = [9, 11, 11, 7, 3, 11, 6, 7, 8, 0, 15, 14, 10, 3, 15, 7, 12, 13, 7, 5, 9, 12, 10, 2]
+S_COLS = {23: 128, 22: 256}
+PE_COLS = {(0, 1): 512, (1, 1): 512, (2, 1): 512, (3, 1): 512, (4, 1): 512, (5, 1): 512, (1, 0): 512, (3, 0): 512, (5, 0): 512, (4, 0): 256}
 B_AFTER = {3: [(0, 0)], 5: [(0, 1)]}
 
 
@@ -111,11 +109,7 @@ def tile_fp8_linear_attention_state_d4_kernel(
             return PE_COLS.get((a, b), 0) if kind == "v" else 0
 
         def n_vec(i):
-            if i == 0:
-                return NV_FIRST
-            if pe_cols(i):
-                return NV_PE
-            return NV_VE if i < N_LATE else max(0, NV_LATE - (i - N_LATE))
+            return NV[i]
 
         def jobs(u):
             kind, a, b = u
@@ -162,17 +156,23 @@ def tile_fp8_linear_attention_state_d4_kernel(
                 b_t = ring([P, 256, 4], BF16)
                 for c1 in range(0, 256, P):
                     nc.tensor.matmul(
-                        out=b_t[:, c1 : c1 + P, :].rearrange("p c t -> p (c t)"),
+                        out=b_t[:, c1 : c1 + P, :].rearrange("p c t -> p t c"),
                         lhsT=ident_b[:],
-                        rhs=wide[i][:, :, c0 + c1 : c0 + c1 + P].rearrange("p t c -> p c t"),
+                        rhs=wide[i][:, :, c0 + c1 : c0 + c1 + P],
                         start=True,
                         stop=True,
                     )
                 nc.scalar.copy(out=gt[:, c0 : c0 + 256, :], in_=b_t[:])
-            if by_pe < HALF:
+            by_s = S_COLS.get(i, 0)
+            if by_s:
+                nc.scalar.copy(
+                    out=gt[:, by_pe : by_pe + by_s, :].rearrange("p (c i) t -> p c t i", i=4),
+                    in_=wide[i][:, :, by_pe : by_pe + by_s].rearrange("p t (c i) -> p c t i", i=4),
+                )
+            if by_pe + by_s < HALF:
                 nc.vector.tensor_copy(
-                    out=gt[:, by_pe:, :].rearrange("p (c i) t -> p c t i", i=4),
-                    in_=wide[i][:, :, by_pe:].rearrange("p t (c i) -> p c t i", i=4),
+                    out=gt[:, by_pe + by_s :, :].rearrange("p (c i) t -> p c t i", i=4),
+                    in_=wide[i][:, :, by_pe + by_s :].rearrange("p t (c i) -> p c t i", i=4),
                 )
 
         def quantise(i):

@@ -22,12 +22,11 @@ P = 128
 PASSES = T // 512
 HALF = 512
 LEAD = 2
-QLAG = 3
+QLAG = 2
 LEAVE = ("ssss", "ssss", "ssss", "vsvs")
 TURNED = "ssss"
-NV = [9, 11, 11, 7, 3, 11, 6, 7, 8, 0, 15, 14, 10, 3, 15, 7, 12, 13, 7, 5, 9, 12, 10, 2]
-S_COLS = {23: 128, 22: 256}
-PE_COLS = {(0, 1): 512, (1, 1): 512, (2, 1): 512, (3, 1): 512, (4, 1): 512, (5, 1): 512, (1, 0): 512, (3, 0): 512, (5, 0): 512, (4, 0): 256}
+NV = [8] + [4] * 23
+S_COLS = {23: 256}
 B_AFTER = {3: [(0, 0)], 5: [(0, 1)]}
 
 
@@ -52,8 +51,9 @@ def tile_fp8_linear_attention_state_d4_kernel(
         def load_scales(first, last):
             k_sc = keep.tile([P, last - first, 16], F32, name="k_sc%d" % first)
             v_sc = keep.tile([P, last - first, 32], F32, name="v_sc%d" % first)
-            nc.sync.dma_start(out=k_sc[:], in_=ks_view[:, first:last, :])
-            nc.sync.dma_start(out=v_sc[:], in_=vs_view[:, first:last, :])
+            queue = nc.scalar if first == 0 else nc.sync
+            queue.dma_start(out=k_sc[:], in_=ks_view[:, first:last, :])
+            queue.dma_start(out=v_sc[:], in_=vs_view[:, first:last, :])
             for g in range(first, last):
                 kscales[g] = k_sc[:, g - first, :]
                 vscales[g] = v_sc[:, g - first, :]
@@ -79,9 +79,7 @@ def tile_fp8_linear_attention_state_d4_kernel(
 
         wsc = keep.tile([P, 2, N], U8, name="wsc", align_bytes=64)
         ident = keep.tile([P, P], F32, name="ident")
-        ident_b = keep.tile([P, P], BF16, name="ident_b")
         dec_sq = keep.tile([P, P], F32, name="dec_sq")
-        make_identity(nc, ident_b[:])
         make_identity(nc, ident[:])
         nc.gpsimd.memset(dec_sq[:], 0.0)
         nc.gpsimd.memset(wsc[:].rearrange("p g n -> p (g n)").bitcast(I32), 0)
@@ -103,10 +101,6 @@ def tile_fp8_linear_attention_state_d4_kernel(
         for g in range(PASSES):
             units += [("k", g, 0), ("v", g, 0), ("v", g, 1)]
         n_units = len(units)
-
-        def pe_cols(i):
-            kind, a, b = units[i]
-            return PE_COLS.get((a, b), 0) if kind == "v" else 0
 
         def n_vec(i):
             return NV[i]
@@ -151,28 +145,16 @@ def tile_fp8_linear_attention_state_d4_kernel(
         def interleave(i):
             gt = stage.tile([P, HALF, 4], BF16, name="gt", bufs=6, align_bytes=64)
             grp[i] = gt
-            by_pe = pe_cols(i)
-            for c0 in range(0, by_pe, 256):
-                b_t = ring([P, 256, 4], BF16)
-                for c1 in range(0, 256, P):
-                    nc.tensor.matmul(
-                        out=b_t[:, c1 : c1 + P, :].rearrange("p c t -> p t c"),
-                        lhsT=ident_b[:],
-                        rhs=wide[i][:, :, c0 + c1 : c0 + c1 + P],
-                        start=True,
-                        stop=True,
-                    )
-                nc.scalar.copy(out=gt[:, c0 : c0 + 256, :], in_=b_t[:])
             by_s = S_COLS.get(i, 0)
             if by_s:
                 nc.scalar.copy(
-                    out=gt[:, by_pe : by_pe + by_s, :].rearrange("p (c i) t -> p c t i", i=4),
-                    in_=wide[i][:, :, by_pe : by_pe + by_s].rearrange("p t (c i) -> p c t i", i=4),
+                    out=gt[:, :by_s, :].rearrange("p (c i) t -> p c t i", i=4),
+                    in_=wide[i][:, :, :by_s].rearrange("p t (c i) -> p c t i", i=4),
                 )
-            if by_pe + by_s < HALF:
+            if by_s < HALF:
                 nc.vector.tensor_copy(
-                    out=gt[:, by_pe + by_s :, :].rearrange("p (c i) t -> p c t i", i=4),
-                    in_=wide[i][:, :, by_pe + by_s :].rearrange("p t (c i) -> p c t i", i=4),
+                    out=gt[:, by_s :, :].rearrange("p (c i) t -> p c t i", i=4),
+                    in_=wide[i][:, :, by_s :].rearrange("p t (c i) -> p c t i", i=4),
                 )
 
         def quantise(i):
@@ -203,7 +185,7 @@ def tile_fp8_linear_attention_state_d4_kernel(
 
         ready = set()
         issued = set()
-        allowed = {0, 1, 2}
+        allowed = {0, 1, 2, 3}
 
         def multiply(i):
             kind, a, b = units[i]
@@ -309,7 +291,6 @@ def tile_fp8_linear_attention_state_d4_kernel(
                 sl = slice((n - 1) * HALF, (n + 1) * HALF)
                 nc.sync.dma_start(out=y_out[dt * P : dt * P + P, sl], in_=yo[dt][:, sl])
 
-        pe_last = max(i for i in range(n_units) if pe_cols(i))
         for i in range(n_units + LEAD + QLAG):
             if i < n_units:
                 widen(i)
@@ -320,8 +301,6 @@ def tile_fp8_linear_attention_state_d4_kernel(
             j = i - LEAD
             if 0 <= j < n_units:
                 interleave(j)
-                if j == pe_last:
-                    allowed.add(3)
             j = i - LEAD - QLAG
             if 0 <= j:
                 quantise(j)

@@ -3,8 +3,8 @@ from contextlib import ExitStack
 import concourse.mybir as mybir
 from concourse.masks import make_identity
 
-T, D, E, N = 4096, 512, 1024, 2048
-FLOPS = 2 * T * D * E + 2 * D * E * N
+TOKENS, KEYS, VALS, OUTS = 4096, 512, 1024, 2048
+FLOPS = 2 * TOKENS * KEYS * VALS + 2 * KEYS * VALS * OUTS
 
 F32 = mybir.dt.float32
 BF16 = mybir.dt.bfloat16
@@ -19,15 +19,22 @@ ADD = mybir.AluOpType.add
 COPY = mybir.ActivationFunctionType.Copy
 
 P = 128
-PASSES = T // 512
+PACK = 4
+PASSES = TOKENS // (P * PACK)
 HALF = 512
-LEAD = 2
-QLAG = 2
-LEAVE = ("ssss", "ssss", "ssss", "vsvs")
-TURNED = "ssss"
-NV = [8] + [4] * 23
-S_COLS = {23: 256}
-B_AFTER = {3: [(0, 0)], 5: [(0, 1)]}
+BLOCKS = HALF // P
+KEY_TILES = KEYS // P
+HALVES = VALS // HALF
+
+UNITS = [(kind, g) for g in range(PASSES) for kind in ("keys", 0, 1)]
+LEAD = 3
+QUANTISE_LAG = 2
+TENSOR_PASSES = 6
+CHUNK = 256
+LATE = len(UNITS) - 2
+SCALAR_COLUMNS = 256
+
+VECTOR_FIRST, VECTOR_TENSOR, VECTOR_PLAIN, VECTOR_LATE = 9, 8, 4, 1
 
 
 def tile_fp8_linear_attention_state_d4_kernel(
@@ -36,306 +43,289 @@ def tile_fp8_linear_attention_state_d4_kernel(
     nc = tc.nc
     with ExitStack() as ctx:
         keep = ctx.enter_context(tc.tile_pool(name="keep", bufs=1))
-        raw = ctx.enter_context(tc.tile_pool(name="raw", bufs=8))
-        stage = ctx.enter_context(tc.tile_pool(name="stage", bufs=3))
-        post = ctx.enter_context(tc.tile_pool(name="post", bufs=2))
+        raw = ctx.enter_context(tc.tile_pool(name="raw", bufs=PASSES))
+        stage = ctx.enter_context(tc.tile_pool(name="stage", bufs=5))
+        post = ctx.enter_context(tc.tile_pool(name="post", bufs=4))
         psum = ctx.enter_context(tc.psum_pool(name="psum", bufs=1))
         ctx.enter_context(tc.manual_schedule())
 
-        kb_view = keys_bytes.rearrange("(g p t) c -> g p t c", p=P, t=4)
-        vb_view = vals_bytes.rearrange("(g p t) c -> g p t c", p=P, t=4)
-        ks_view = keys_scale.rearrange("(g p t) b -> p g (t b)", p=P, t=4)
-        vs_view = vals_scale.rearrange("(g p t) b -> p g (t b)", p=P, t=4)
-        kbytes, vbytes, kscales, vscales = [], [], {}, {}
+        keys_view = keys_bytes.rearrange("(g p t) c -> g p t c", p=P, t=PACK)
+        vals_view = vals_bytes.rearrange("(g p t) c -> g p t c", p=P, t=PACK)
+        keys_scale_view = keys_scale.rearrange("(g p t) b -> p g (t b)", p=P, t=PACK)
+        vals_scale_view = vals_scale.rearrange("(g p t) b -> p g (t b)", p=P, t=PACK)
+        key_raw, val_raw, key_scale_of, val_scale_of = [], [], {}, {}
 
-        def load_scales(first, last):
-            k_sc = keep.tile([P, last - first, 16], F32, name="k_sc%d" % first)
-            v_sc = keep.tile([P, last - first, 32], F32, name="v_sc%d" % first)
-            queue = nc.scalar if first == 0 else nc.sync
-            queue.dma_start(out=k_sc[:], in_=ks_view[:, first:last, :])
-            queue.dma_start(out=v_sc[:], in_=vs_view[:, first:last, :])
+        def load_scales(first, last, queue):
+            key_sc = keep.tile([P, last - first, PACK * KEYS // P], F32, name="key_sc%d" % first)
+            val_sc = keep.tile([P, last - first, PACK * VALS // P], F32, name="val_sc%d" % first)
+            queue.dma_start(out=key_sc[:], in_=keys_scale_view[:, first:last, :])
+            queue.dma_start(out=val_sc[:], in_=vals_scale_view[:, first:last, :])
             for g in range(first, last):
-                kscales[g] = k_sc[:, g - first, :]
-                vscales[g] = v_sc[:, g - first, :]
+                key_scale_of[g] = key_sc[:, g - first, :]
+                val_scale_of[g] = val_sc[:, g - first, :]
 
-        dec_rows = keep.tile([4, P], BF16, name="dec_rows")
+        decay_rows = keep.tile([KEY_TILES, P], BF16, name="decay_rows")
         for g in range(PASSES):
-            if g < 2:
-                load_scales(g, g + 1)
-            kb = raw.tile([P, 4, D], U8, name="kb")
-            nc.sync.dma_start(out=kb[:], in_=kb_view[g])
-            vb = raw.tile([P, 4, E], U8, name="vb")
-            nc.sync.dma_start(out=vb[:], in_=vb_view[g])
             if g == 0:
-                nc.sync.dma_start(out=dec_rows[:], in_=decay.rearrange("(d p) -> d p", p=P))
-            if g == 1:
-                load_scales(2, PASSES)
-            kbytes.append(kb)
-            vbytes.append(vb)
-        prev = keep.tile([P, 4, E], BF16, name="prev")
+                load_scales(0, 1, nc.scalar)
+            elif g == 1:
+                load_scales(1, 2, nc.sync)
+            key_bytes = raw.tile([P, PACK, KEYS], U8, name="key_bytes")
+            nc.sync.dma_start(out=key_bytes[:], in_=keys_view[g])
+            val_bytes = raw.tile([P, PACK, VALS], U8, name="val_bytes")
+            nc.sync.dma_start(out=val_bytes[:], in_=vals_view[g])
+            key_raw.append(key_bytes)
+            val_raw.append(val_bytes)
+            if g == 0:
+                nc.sync.dma_start(out=decay_rows[:], in_=decay.rearrange("(d p) -> d p", p=P))
+            elif g == 1:
+                load_scales(2, PASSES, nc.sync)
+        prev = keep.tile([P, KEY_TILES, VALS], BF16, name="prev")
         nc.sync.dma_start(out=prev[:], in_=prev_state.rearrange("(d p) e -> p d e", p=P))
-        gain_b = keep.tile([P, E], BF16, name="gain_b")
-        nc.sync.dma_start(out=gain_b[:], in_=gain.partition_broadcast(P))
+        gain_rows = keep.tile([P, VALS], BF16, name="gain_rows")
+        nc.sync.dma_start(out=gain_rows[:], in_=gain.partition_broadcast(P))
 
-        wsc = keep.tile([P, 2, N], U8, name="wsc", align_bytes=64)
         ident = keep.tile([P, P], F32, name="ident")
-        dec_sq = keep.tile([P, P], F32, name="dec_sq")
+        ident_bf = keep.tile([P, P], BF16, name="ident_bf")
+        decay_square = keep.tile([P, P], F32, name="decay_square")
+        w_scale_rows = keep.tile([P, 2, OUTS], U8, name="w_scale_rows", align_bytes=64)
+        make_identity(nc, ident_bf[:])
         make_identity(nc, ident[:])
-        nc.gpsimd.memset(dec_sq[:], 0.0)
-        nc.gpsimd.memset(wsc[:].rearrange("p g n -> p (g n)").bitcast(I32), 0)
+        nc.gpsimd.memset(decay_square[:], 0.0)
+        nc.gpsimd.memset(w_scale_rows[:].rearrange("p g n -> p (g n)").bitcast(I32), 0)
         for q in range(4):
             nc.sync.dma_start(
-                out=wsc[32 * q : 32 * q + 4].bitcast(I32),
+                out=w_scale_rows[32 * q : 32 * q + 4].bitcast(I32),
                 in_=w_scales[:, 4 * q : 4 * q + 4, :].rearrange("g q n -> q g n").bitcast(I32),
             )
-        ww = keep.tile([P, 2, 2 * N], U8, name="ww", align_bytes=64)
+        w_codes = keep.tile([P, 2, 2 * OUTS], U8, name="w_codes", align_bytes=64)
         for g in range(2):
-            nc.sync.dma_start(out=ww[:, g, :].bitcast(I32), in_=w_words[g].bitcast(I32))
+            nc.sync.dma_start(out=w_codes[:, g, :].bitcast(I32), in_=w_words[g].bitcast(I32))
 
-        vc = keep.tile([P, PASSES, E], U32, name="vc", align_bytes=64)
-        vpl = keep.tile([P, PASSES, E], U8, name="vpl", align_bytes=64)
-        ka = keep.tile([P, PASSES, D], U32, name="ka", align_bytes=64)
-        kapl = keep.tile([P, PASSES, D], U8, name="kapl", align_bytes=64)
+        key_codes = keep.tile([P, PASSES, KEYS], U32, name="key_codes", align_bytes=64)
+        key_planes = keep.tile([P, PASSES, KEYS], U8, name="key_planes", align_bytes=64)
+        val_codes = keep.tile([P, PASSES, VALS], U32, name="val_codes", align_bytes=64)
+        val_planes = keep.tile([P, PASSES, VALS], U8, name="val_planes", align_bytes=64)
+        wide, grouped = {}, {}
 
-        units = []
-        for g in range(PASSES):
-            units += [("k", g, 0), ("v", g, 0), ("v", g, 1)]
-        n_units = len(units)
+        def bank(b, shape, dtype):
+            return psum.tile(shape, dtype, name="bank%d" % b)
 
-        def n_vec(i):
-            return NV[i]
+        def on_tensor(i):
+            kind, g = UNITS[i]
+            return kind == 1 and g < TENSOR_PASSES
 
-        def jobs(u):
-            kind, a, b = u
-            out = []
-            if kind == "k":
-                for blk in range(4):
-                    for t in range(4):
-                        out.append((kbytes[a][:, t, blk * P : blk * P + P], t, blk, kscales[a][:, 4 * t + blk : 4 * t + blk + 1]))
-            else:
-                for blk in range(4):
-                    for t in range(4):
-                        c = b * 4 + blk
-                        out.append((vbytes[a][:, t, c * P : c * P + P], t, blk, vscales[a][:, 8 * t + c : 8 * t + c + 1]))
-            return out
+        last_on_tensor = max(i for i in range(len(UNITS)) if on_tensor(i))
 
-        banks = {"next": 0, "ring": [6, 7]}
-
-        def bank(b, shape, dt):
-            return psum.tile(shape, dt, name="bank%d" % b)
-
-        def ring(shape, dt):
-            b = banks["ring"][banks["next"] % len(banks["ring"])]
-            banks["next"] += 1
-            return bank(b, shape, dt)
-
-        wide, grp, lain = {}, {}, {}
+        def vector_widens(i):
+            if i == 0:
+                return VECTOR_FIRST
+            if i >= LATE:
+                return VECTOR_LATE
+            return VECTOR_TENSOR if on_tensor(i) else VECTOR_PLAIN
 
         def widen(i):
-            js = jobs(units[i])
-            w = stage.tile([P, 4, HALF], BF16, name="w", bufs=6, align_bytes=64)
-            wide[i] = w
-            for k, (src, t, blk, sc) in enumerate(js):
-                dst = w[:, t, blk * P : blk * P + P]
-                if k < n_vec(i):
-                    nc.vector.tensor_scalar(out=dst, in0=src.bitcast(F8), scalar1=sc, scalar2=None, op0=MULT)
+            kind, g = UNITS[i]
+            w_t = stage.tile([P, PACK, HALF], BF16, name="w_t", align_bytes=64)
+            wide[i] = w_t
+            for n in range(BLOCKS * PACK):
+                blk, t = divmod(n, PACK)
+                if kind == "keys":
+                    source = key_raw[g][:, t, blk * P : blk * P + P]
+                    at = t * (KEYS // P) + blk
+                    scale = key_scale_of[g][:, at : at + 1]
                 else:
-                    nc.scalar.activation(out=dst, in_=src.bitcast(F8), func=COPY, scale=sc)
+                    block = kind * BLOCKS + blk
+                    source = val_raw[g][:, t, block * P : block * P + P]
+                    at = t * (VALS // P) + block
+                    scale = val_scale_of[g][:, at : at + 1]
+                target = w_t[:, t, blk * P : blk * P + P]
+                if n < vector_widens(i):
+                    nc.vector.tensor_scalar(out=target, in0=source.bitcast(F8), scalar1=scale, scalar2=None, op0=MULT)
+                else:
+                    nc.scalar.activation(out=target, in_=source.bitcast(F8), func=COPY, scale=scale)
 
         def interleave(i):
-            gt = stage.tile([P, HALF, 4], BF16, name="gt", bufs=6, align_bytes=64)
-            grp[i] = gt
-            by_s = S_COLS.get(i, 0)
-            if by_s:
+            g_t = stage.tile([P, HALF, PACK], BF16, name="g_t", align_bytes=64)
+            grouped[i] = g_t
+            if on_tensor(i):
+                for c0 in range(0, HALF, CHUNK):
+                    laid = bank(6 + c0 // CHUNK, [P, CHUNK, PACK], BF16)
+                    for c1 in range(0, CHUNK, P):
+                        nc.tensor.matmul(
+                            out=laid[:, c1 : c1 + P, :].rearrange("p c t -> p t c"),
+                            lhsT=ident_bf[:],
+                            rhs=wide[i][:, :, c0 + c1 : c0 + c1 + P],
+                            start=True,
+                            stop=True,
+                        )
+                    nc.scalar.copy(out=g_t[:, c0 : c0 + CHUNK, :], in_=laid[:])
+                return
+            split = SCALAR_COLUMNS if i >= LATE else 0
+            if split:
                 nc.scalar.copy(
-                    out=gt[:, :by_s, :].rearrange("p (c i) t -> p c t i", i=4),
-                    in_=wide[i][:, :, :by_s].rearrange("p t (c i) -> p c t i", i=4),
+                    out=g_t[:, :split, :].rearrange("p (c i) t -> p c t i", i=4),
+                    in_=wide[i][:, :, :split].rearrange("p t (c i) -> p c t i", i=4),
                 )
-            if by_s < HALF:
-                nc.vector.tensor_copy(
-                    out=gt[:, by_s :, :].rearrange("p (c i) t -> p c t i", i=4),
-                    in_=wide[i][:, :, by_s :].rearrange("p t (c i) -> p c t i", i=4),
-                )
+            nc.vector.tensor_copy(
+                out=g_t[:, split:, :].rearrange("p (c i) t -> p c t i", i=4),
+                in_=wide[i][:, :, split:].rearrange("p t (c i) -> p c t i", i=4),
+            )
 
         def quantise(i):
-            kind, a, b = units[i]
-            if kind == "k":
-                co, pl = ka[:, a, :], kapl[:, a, :]
+            kind, g = UNITS[i]
+            if kind == "keys":
+                codes, plane = key_codes[:, g, :], key_planes[:, g, :]
             else:
-                co, pl = vc[:, a, b * HALF : b * HALF + HALF], vpl[:, a, b * HALF : b * HALF + HALF]
-            nc.vector.quantize_mx(out=co.bitcast(FP8X4), scales=pl, in_=grp[i][:].rearrange("p c t -> p (c t)"))
+                columns = slice(kind * HALF, kind * HALF + HALF)
+                codes, plane = val_codes[:, g, columns], val_planes[:, g, columns]
+            nc.vector.quantize_mx(
+                out=codes.bitcast(FP8X4), scales=plane, in_=grouped[i][:].rearrange("p c t -> p (c t)")
+            )
 
         kv = {}
-        KV_BANK = {(dt, eh): 2 * dt + eh for dt in range(4) for eh in range(2)}
+        waiting = []
 
-        def mm(dt, eh, g):
+        def product(d, e, g):
             if g == 0:
-                acc = bank(KV_BANK[dt, eh], [P, HALF], F32)
-                kv[dt, eh] = acc
-            lc, lp = ka[:, g, dt * P : dt * P + P], kapl[:, g, dt * P : dt * P + P]
+                acc = bank(2 * d + e, [P, HALF], F32)
+                kv[d, e] = acc
+            rows = slice(d * P, d * P + P)
+            columns = slice(e * HALF, e * HALF + HALF)
             nc.tensor.matmul_mx(
-                out=kv[dt, eh][:],
-                lhsT=lc.bitcast(FP8X4),
-                lhsT_scale=lp,
-                rhs=vc[:, g, eh * HALF : eh * HALF + HALF].bitcast(FP8X4),
-                rhs_scale=vpl[:, g, eh * HALF : eh * HALF + HALF],
+                out=kv[d, e][:],
+                lhsT=key_codes[:, g, rows].bitcast(FP8X4),
+                lhsT_scale=key_planes[:, g, rows],
+                rhs=val_codes[:, g, columns].bitcast(FP8X4),
+                rhs_scale=val_planes[:, g, columns],
                 start=(g == 0),
                 stop=(g == PASSES - 1),
             )
 
-        ready = set()
-        issued = set()
-        allowed = {0, 1, 2, 3}
+        def multiply(i, last_tile_may_run):
+            kind, g = UNITS[i]
+            if kind != "keys":
+                for d in range(KEY_TILES - 1):
+                    product(d, kind, g)
+                waiting.append((kind, g))
+            if last_tile_may_run:
+                for e, g_done in sorted(waiting):
+                    product(KEY_TILES - 1, e, g_done)
+                waiting.clear()
 
-        def multiply(i):
-            kind, a, b = units[i]
-            if kind == "v":
-                ready.add(("v", b, a))
-            else:
-                ready.update([(dt, a) for dt in range(4)])
-            issue()
+        decay_cols = keep.tile([P, KEY_TILES], F32, name="decay_cols")
 
-        def issue():
-            for dt in sorted(allowed):
-                for eh in range(2):
-                    for g in range(PASSES):
-                        key = (dt, eh, g)
-                        if key in issued:
-                            continue
-                        if (dt, g) in ready and ("v", eh, g) in ready:
-                            mm(dt, eh, g)
-                            issued.add(key)
-                        else:
-                            break
+        def turn_decay():
+            nc.scalar.copy(out=decay_square[0:KEY_TILES, :], in_=decay_rows[:])
+            turned_decay = bank(0, [P, P], F32)
+            nc.tensor.transpose(turned_decay[:], decay_square[:], ident[:])
+            return turned_decay
 
-        dec_c = keep.tile([P, 4], F32, name="dec_c")
-
-        def decay_square():
-            nc.scalar.copy(out=dec_sq[0:4, :], in_=dec_rows[:])
-            dt_ps = bank(0, [P, P], F32)
-            nc.tensor.transpose(dt_ps[:], dec_sq[:], ident[:])
-            return dt_ps
-
-        def decay_columns(dt_ps):
-            nc.scalar.copy(out=dec_c[:], in_=dt_ps[:, 0:4])
-
-        st, hb, xt, hg, hc, hp, ys, yo = {}, {}, {}, {}, {}, {}, {}, {}
-
-        def state(dt, eh):
-            if eh == 0:
-                s_t = post.tile([P, E], F32, name="s_t", bufs=3)
-                st[dt] = s_t
-            sl = slice(eh * HALF, eh * HALF + HALF)
-            nc.vector.scalar_tensor_tensor(
-                out=st[dt][:, sl], in0=prev[:, dt, sl], scalar=dec_c[:, dt : dt + 1], in1=kv[dt, eh][:], op0=MULT, op1=ADD
-            )
-            if eh == 1:
-                nc.sync.dma_start(out=state_out[dt * P : dt * P + P, :], in_=st[dt][:])
-
-        def gained(dt, eh):
-            if eh == 0:
-                h_t = post.tile([P, E], BF16, name="h_t")
-                hb[dt] = h_t
-            sl = slice(eh * HALF, eh * HALF + HALF)
-            nc.vector.tensor_tensor(out=hb[dt][:, sl], in0=st[dt][:, sl], in1=gain_b[:, sl], op=MULT)
-
-        def turn(dt, g):
-            x_t = ring([P, 2, P], F32)
-            xt[dt, g] = x_t
-            words = hb[dt][:].bitcast(F32)
-            for u in range(2):
-                nc.tensor.transpose(x_t[:, u, :], words[:, 256 * g + u : 256 * (g + 1) : 2], ident[:])
-
-        def turned(dt, g, eng="s"):
-            g_t = post.tile([P, P, 4], BF16, name="g_t", bufs=4, align_bytes=64)
-            hg[dt, g] = g_t
-            dst = g_t[:].rearrange("p r t -> p (r t)").bitcast(F32).rearrange("p (r u) -> p r u", u=2)
-            src = xt[dt, g][:].rearrange("p u r -> p r u")
-            if eng == "s":
-                nc.scalar.copy(out=dst, in_=src)
-            else:
-                nc.vector.tensor_copy(out=dst, in_=src)
-
-        def quantise_h(dt, g):
-            c_t = post.tile([P, P], U32, name="c_t", bufs=4, align_bytes=64)
-            p_t = post.tile([P, P], U8, name="p_t", bufs=4, align_bytes=64)
-            hc[dt, g], hp[dt, g] = c_t, p_t
-            nc.vector.quantize_mx(
-                out=c_t[:].bitcast(FP8X4), scales=p_t[:], in_=hg[dt, g][:].rearrange("p r t -> p (r t)")
-            )
-
-        def project(dt, n, g):
-            if g == 0:
-                y_p = ring([P, HALF], F32)
-                ys[dt, n] = y_p
-            nc.tensor.matmul_mx(
-                out=ys[dt, n][:],
-                lhsT=hc[dt, g][:].bitcast(FP8X4),
-                lhsT_scale=hp[dt, g][:],
-                rhs=ww[:, g, n * 1024 : n * 1024 + 1024].bitcast(FP4X4),
-                rhs_scale=wsc[:, g, n * HALF : n * HALF + HALF],
-                start=(g == 0),
-                stop=(g == 1),
-            )
-
-        def leave(dt, n, eng):
-            if n == 0:
-                y_t = post.tile([P, N], F32, name="y_t", bufs=3)
-                yo[dt] = y_t
-            dst = yo[dt][:, n * HALF : n * HALF + HALF]
-            if eng == "s":
-                nc.scalar.copy(out=dst, in_=ys[dt, n][:])
-            else:
-                nc.vector.tensor_copy(out=dst, in_=ys[dt, n][:])
-            if n % 2 == 1:
-                sl = slice((n - 1) * HALF, (n + 1) * HALF)
-                nc.sync.dma_start(out=y_out[dt * P : dt * P + P, sl], in_=yo[dt][:, sl])
-
-        for i in range(n_units + LEAD + QLAG):
-            if i < n_units:
+        for i in range(len(UNITS) + LEAD + QUANTISE_LAG):
+            if i < len(UNITS):
                 widen(i)
-            if i == 3:
-                turned_decay = decay_square()
-            if i == 4:
-                decay_columns(turned_decay)
-            j = i - LEAD
-            if 0 <= j < n_units:
-                interleave(j)
-            j = i - LEAD - QLAG
-            if 0 <= j:
-                quantise(j)
-                multiply(j)
+            if i == LEAD:
+                decay_in_psum = turn_decay()
+            if i == LEAD + 1:
+                nc.scalar.copy(out=decay_cols[:], in_=decay_in_psum[:, 0:KEY_TILES])
+            if 0 <= i - LEAD < len(UNITS):
+                interleave(i - LEAD)
+            if i >= LEAD + QUANTISE_LAG:
+                quantise(i - LEAD - QUANTISE_LAG)
+                multiply(i - LEAD - QUANTISE_LAG, i - LEAD >= last_on_tensor)
 
-        def turns(dt):
-            turn(dt, 0)
-            turn(dt, 1)
-            turned(dt, 0, TURNED[dt])
-            turned(dt, 1, TURNED[dt])
+        free_banks, held_bank = [], {}
+        state_of, h_of, turned, h_grouped, h_codes, h_planes, y_psum, y_of = {}, {}, {}, {}, {}, {}, {}, {}
 
-        def projects(dt, first):
-            for n in (first, first + 1):
-                project(dt, n, 0)
-                project(dt, n, 1)
-                leave(dt, n, LEAVE[dt][n])
+        def take_bank(holder, shape):
+            held_bank[holder] = free_banks.pop(0)
+            return bank(held_bank[holder], shape, F32)
 
-        banks["ring"] = [0, 2, 1, 3, 4, 5, 6, 7]
-        banks["next"] = 0
+        def state(d, e):
+            if d not in state_of:
+                s_t = post.tile([P, VALS], F32, name="s_t")
+                state_of[d] = s_t
+            columns = slice(e * HALF, e * HALF + HALF)
+            nc.vector.scalar_tensor_tensor(
+                out=state_of[d][:, columns],
+                in0=prev[:, d, columns],
+                scalar=decay_cols[:, d : d + 1],
+                in1=kv[d, e][:],
+                op0=MULT,
+                op1=ADD,
+            )
+            free_banks.append(2 * d + e)
+            if e == HALVES - 1:
+                nc.sync.dma_start(out=state_out[d * P : d * P + P, :], in_=state_of[d][:])
+
+        def gained(d):
+            h_t = post.tile([P, VALS], BF16, name="h_t", bufs=2)
+            h_of[d] = h_t
+            for e in range(HALVES):
+                columns = slice(e * HALF, e * HALF + HALF)
+                nc.vector.tensor_tensor(
+                    out=h_t[:, columns], in0=state_of[d][:, columns], in1=gain_rows[:, columns], op=MULT
+                )
+
+        def turn(d):
+            words = h_of[d][:].bitcast(F32)
+            for g in range(2):
+                x_t = take_bank(("turned", d, g), [P, 2, P])
+                turned[d, g] = x_t
+                for u in range(2):
+                    nc.tensor.transpose(x_t[:, u, :], words[:, 256 * g + u : 256 * (g + 1) : 2], ident[:])
+            for g in range(2):
+                hg_t = post.tile([P, P, PACK], BF16, name="hg_t", align_bytes=64)
+                h_grouped[d, g] = hg_t
+                pairs = hg_t[:].rearrange("p r t -> p (r t)").bitcast(F32)
+                nc.scalar.copy(
+                    out=pairs.rearrange("p (r u) -> p r u", u=2), in_=turned[d, g][:].rearrange("p u r -> p r u")
+                )
+                free_banks.append(held_bank["turned", d, g])
+
+        def quantise_h(d):
+            for g in range(2):
+                hc_t = post.tile([P, P], U32, name="hc_t", align_bytes=64)
+                hp_t = post.tile([P, P], U8, name="hp_t", align_bytes=64)
+                h_codes[d, g], h_planes[d, g] = hc_t, hp_t
+                nc.vector.quantize_mx(
+                    out=hc_t[:].bitcast(FP8X4), scales=hp_t[:], in_=h_grouped[d, g][:].rearrange("p r t -> p (r t)")
+                )
+
+        def project(d, n, engine_copy):
+            if d not in y_of:
+                y_t = post.tile([P, OUTS], F32, name="y_t", bufs=3)
+                y_of[d] = y_t
+            y_p = take_bank(("y", d, n), [P, HALF])
+            columns = slice(n * HALF, n * HALF + HALF)
+            for g in range(2):
+                nc.tensor.matmul_mx(
+                    out=y_p[:],
+                    lhsT=h_codes[d, g][:].bitcast(FP8X4),
+                    lhsT_scale=h_planes[d, g][:],
+                    rhs=w_codes[:, g, 2 * n * HALF : 2 * (n + 1) * HALF].bitcast(FP4X4),
+                    rhs_scale=w_scale_rows[:, g, columns],
+                    start=(g == 0),
+                    stop=(g == 1),
+                )
+            engine_copy(out=y_of[d][:, columns], in_=y_p[:])
+            free_banks.append(held_bank["y", d, n])
+            nc.sync.dma_start(out=y_out[d * P : d * P + P, columns], in_=y_of[d][:, columns])
+
         state(0, 0)
         state(1, 0)
         state(0, 1)
-        gained(0, 0)
-        gained(0, 1)
-        turns(0)
+        gained(0)
+        turn(0)
         state(1, 1)
-        for dt in range(4):
-            quantise_h(dt, 0)
-            quantise_h(dt, 1)
-            projects(dt, 0)
-            if dt < 3:
-                gained(dt + 1, 0)
-                gained(dt + 1, 1)
-                turns(dt + 1)
-            if dt < 2:
-                state(dt + 2, 0)
-                state(dt + 2, 1)
-            projects(dt, 2)
+        for d in range(KEY_TILES):
+            quantise_h(d)
+            for n in range(OUTS // HALF):
+                if n == 2 and d + 1 < KEY_TILES:
+                    gained(d + 1)
+                    turn(d + 1)
+                    if d + 2 < KEY_TILES:
+                        state(d + 2, 0)
+                        state(d + 2, 1)
+                on_vector = d == KEY_TILES - 1 and n % 2 == 0
+                project(d, n, nc.vector.tensor_copy if on_vector else nc.scalar.copy)

from contextlib import ExitStack

import concourse.mybir as mybir
from concourse.masks import make_identity

TOKENS, KEYS, VALS, OUTS = 4096, 512, 1024, 2048
FLOPS = 2 * TOKENS * KEYS * VALS + 2 * KEYS * VALS * OUTS

F32 = mybir.dt.float32
BF16 = mybir.dt.bfloat16
I32 = mybir.dt.int32
U32 = mybir.dt.uint32
U8 = mybir.dt.uint8
F8 = mybir.dt.float8_e4m3fn
FP8X4 = mybir.dt.float8_e4m3fn_x4
FP4X4 = mybir.dt.float4_e2m1fn_x4
MULT = mybir.AluOpType.mult
ADD = mybir.AluOpType.add
COPY = mybir.ActivationFunctionType.Copy

P = 128
PACK = 4
PASSES = TOKENS // (P * PACK)
HALF = 512
BLOCKS = HALF // P
KEY_TILES = KEYS // P
HALVES = VALS // HALF

UNITS = [(kind, g) for g in range(PASSES) for kind in ("keys", 0, 1)]
LEAD = 3
QUANTISE_LAG = 2
TENSOR_PASSES = 6
CHUNK = 256
LATE = len(UNITS) - 2
SCALAR_COLUMNS = 256

VECTOR_FIRST, VECTOR_TENSOR, VECTOR_PLAIN, VECTOR_LATE = 9, 8, 4, 1


def tile_fp8_linear_attention_state_d4_kernel(
    tc, keys_bytes, keys_scale, vals_bytes, vals_scale, prev_state, decay, gain, w_words, w_scales, state_out, y_out
):
    nc = tc.nc
    with ExitStack() as ctx:
        keep = ctx.enter_context(tc.tile_pool(name="keep", bufs=1))
        raw = ctx.enter_context(tc.tile_pool(name="raw", bufs=PASSES))
        stage = ctx.enter_context(tc.tile_pool(name="stage", bufs=5))
        post = ctx.enter_context(tc.tile_pool(name="post", bufs=4))
        psum = ctx.enter_context(tc.psum_pool(name="psum", bufs=1))
        ctx.enter_context(tc.manual_schedule())

        keys_view = keys_bytes.rearrange("(g p t) c -> g p t c", p=P, t=PACK)
        vals_view = vals_bytes.rearrange("(g p t) c -> g p t c", p=P, t=PACK)
        keys_scale_view = keys_scale.rearrange("(g p t) b -> p g (t b)", p=P, t=PACK)
        vals_scale_view = vals_scale.rearrange("(g p t) b -> p g (t b)", p=P, t=PACK)
        key_raw, val_raw, key_scale_of, val_scale_of = [], [], {}, {}

        def load_scales(first, last, queue):
            key_sc = keep.tile([P, last - first, PACK * KEYS // P], F32, name="key_sc%d" % first)
            val_sc = keep.tile([P, last - first, PACK * VALS // P], F32, name="val_sc%d" % first)
            queue.dma_start(out=key_sc[:], in_=keys_scale_view[:, first:last, :])
            queue.dma_start(out=val_sc[:], in_=vals_scale_view[:, first:last, :])
            for g in range(first, last):
                key_scale_of[g] = key_sc[:, g - first, :]
                val_scale_of[g] = val_sc[:, g - first, :]

        decay_rows = keep.tile([KEY_TILES, P], BF16, name="decay_rows")
        for g in range(PASSES):
            if g == 0:
                load_scales(0, 1, nc.scalar)
            elif g == 1:
                load_scales(1, 2, nc.sync)
            key_bytes = raw.tile([P, PACK, KEYS], U8, name="key_bytes")
            nc.sync.dma_start(out=key_bytes[:], in_=keys_view[g])
            val_bytes = raw.tile([P, PACK, VALS], U8, name="val_bytes")
            nc.sync.dma_start(out=val_bytes[:], in_=vals_view[g])
            key_raw.append(key_bytes)
            val_raw.append(val_bytes)
            if g == 0:
                nc.sync.dma_start(out=decay_rows[:], in_=decay.rearrange("(d p) -> d p", p=P))
            elif g == 1:
                load_scales(2, PASSES, nc.sync)
        prev = keep.tile([P, KEY_TILES, VALS], BF16, name="prev")
        nc.sync.dma_start(out=prev[:], in_=prev_state.rearrange("(d p) e -> p d e", p=P))
        gain_rows = keep.tile([P, VALS], BF16, name="gain_rows")
        nc.sync.dma_start(out=gain_rows[:], in_=gain.partition_broadcast(P))

        ident = keep.tile([P, P], F32, name="ident")
        ident_bf = keep.tile([P, P], BF16, name="ident_bf")
        decay_square = keep.tile([P, P], F32, name="decay_square")
        w_scale_rows = keep.tile([P, 2, OUTS], U8, name="w_scale_rows", align_bytes=64)
        make_identity(nc, ident_bf[:])
        make_identity(nc, ident[:])
        nc.gpsimd.memset(decay_square[:], 0.0)
        nc.gpsimd.memset(w_scale_rows[:].rearrange("p g n -> p (g n)").bitcast(I32), 0)
        for q in range(4):
            nc.sync.dma_start(
                out=w_scale_rows[32 * q : 32 * q + 4].bitcast(I32),
                in_=w_scales[:, 4 * q : 4 * q + 4, :].rearrange("g q n -> q g n").bitcast(I32),
            )
        w_codes = keep.tile([P, 2, 2 * OUTS], U8, name="w_codes", align_bytes=64)
        for g in range(2):
            nc.sync.dma_start(out=w_codes[:, g, :].bitcast(I32), in_=w_words[g].bitcast(I32))

        key_codes = keep.tile([P, PASSES, KEYS], U32, name="key_codes", align_bytes=64)
        key_planes = keep.tile([P, PASSES, KEYS], U8, name="key_planes", align_bytes=64)
        val_codes = keep.tile([P, PASSES, VALS], U32, name="val_codes", align_bytes=64)
        val_planes = keep.tile([P, PASSES, VALS], U8, name="val_planes", align_bytes=64)
        wide, grouped = {}, {}

        def bank(b, shape, dtype):
            return psum.tile(shape, dtype, name="bank%d" % b)

        def on_tensor(i):
            kind, g = UNITS[i]
            return kind == 1 and g < TENSOR_PASSES

        last_on_tensor = max(i for i in range(len(UNITS)) if on_tensor(i))

        def vector_widens(i):
            if i == 0:
                return VECTOR_FIRST
            if i >= LATE:
                return VECTOR_LATE
            return VECTOR_TENSOR if on_tensor(i) else VECTOR_PLAIN

        def widen(i):
            kind, g = UNITS[i]
            w_t = stage.tile([P, PACK, HALF], BF16, name="w_t", align_bytes=64)
            wide[i] = w_t
            for n in range(BLOCKS * PACK):
                blk, t = divmod(n, PACK)
                if kind == "keys":
                    source = key_raw[g][:, t, blk * P : blk * P + P]
                    at = t * (KEYS // P) + blk
                    scale = key_scale_of[g][:, at : at + 1]
                else:
                    block = kind * BLOCKS + blk
                    source = val_raw[g][:, t, block * P : block * P + P]
                    at = t * (VALS // P) + block
                    scale = val_scale_of[g][:, at : at + 1]
                target = w_t[:, t, blk * P : blk * P + P]
                if n < vector_widens(i):
                    nc.vector.tensor_scalar(out=target, in0=source.bitcast(F8), scalar1=scale, scalar2=None, op0=MULT)
                else:
                    nc.scalar.activation(out=target, in_=source.bitcast(F8), func=COPY, scale=scale)

        def interleave(i):
            g_t = stage.tile([P, HALF, PACK], BF16, name="g_t", align_bytes=64)
            grouped[i] = g_t
            if on_tensor(i):
                for c0 in range(0, HALF, CHUNK):
                    laid = bank(6 + c0 // CHUNK, [P, CHUNK, PACK], BF16)
                    for c1 in range(0, CHUNK, P):
                        nc.tensor.matmul(
                            out=laid[:, c1 : c1 + P, :].rearrange("p c t -> p t c"),
                            lhsT=ident_bf[:],
                            rhs=wide[i][:, :, c0 + c1 : c0 + c1 + P],
                            start=True,
                            stop=True,
                        )
                    nc.scalar.copy(out=g_t[:, c0 : c0 + CHUNK, :], in_=laid[:])
                return
            split = SCALAR_COLUMNS if i >= LATE else 0
            if split:
                nc.scalar.copy(
                    out=g_t[:, :split, :].rearrange("p (c i) t -> p c t i", i=4),
                    in_=wide[i][:, :, :split].rearrange("p t (c i) -> p c t i", i=4),
                )
            nc.vector.tensor_copy(
                out=g_t[:, split:, :].rearrange("p (c i) t -> p c t i", i=4),
                in_=wide[i][:, :, split:].rearrange("p t (c i) -> p c t i", i=4),
            )

        def quantise(i):
            kind, g = UNITS[i]
            if kind == "keys":
                codes, plane = key_codes[:, g, :], key_planes[:, g, :]
            else:
                columns = slice(kind * HALF, kind * HALF + HALF)
                codes, plane = val_codes[:, g, columns], val_planes[:, g, columns]
            nc.vector.quantize_mx(
                out=codes.bitcast(FP8X4), scales=plane, in_=grouped[i][:].rearrange("p c t -> p (c t)")
            )

        kv = {}
        waiting = []

        def product(d, e, g):
            if g == 0:
                acc = bank(2 * d + e, [P, HALF], F32)
                kv[d, e] = acc
            rows = slice(d * P, d * P + P)
            columns = slice(e * HALF, e * HALF + HALF)
            nc.tensor.matmul_mx(
                out=kv[d, e][:],
                lhsT=key_codes[:, g, rows].bitcast(FP8X4),
                lhsT_scale=key_planes[:, g, rows],
                rhs=val_codes[:, g, columns].bitcast(FP8X4),
                rhs_scale=val_planes[:, g, columns],
                start=(g == 0),
                stop=(g == PASSES - 1),
            )

        def multiply(i, last_tile_may_run):
            kind, g = UNITS[i]
            if kind != "keys":
                for d in range(KEY_TILES - 1):
                    product(d, kind, g)
                waiting.append((kind, g))
            if last_tile_may_run:
                for e, g_done in sorted(waiting):
                    product(KEY_TILES - 1, e, g_done)
                waiting.clear()

        decay_cols = keep.tile([P, KEY_TILES], F32, name="decay_cols")

        def turn_decay():
            nc.scalar.copy(out=decay_square[0:KEY_TILES, :], in_=decay_rows[:])
            turned_decay = bank(0, [P, P], F32)
            nc.tensor.transpose(turned_decay[:], decay_square[:], ident[:])
            return turned_decay

        for i in range(len(UNITS) + LEAD + QUANTISE_LAG):
            if i < len(UNITS):
                widen(i)
            if i == LEAD:
                decay_in_psum = turn_decay()
            if i == LEAD + 1:
                nc.scalar.copy(out=decay_cols[:], in_=decay_in_psum[:, 0:KEY_TILES])
            if 0 <= i - LEAD < len(UNITS):
                interleave(i - LEAD)
            if i >= LEAD + QUANTISE_LAG:
                quantise(i - LEAD - QUANTISE_LAG)
                multiply(i - LEAD - QUANTISE_LAG, i - LEAD >= last_on_tensor)

        free_banks, held_bank = [], {}
        state_of, h_of, turned, h_grouped, h_codes, h_planes, y_psum, y_of = {}, {}, {}, {}, {}, {}, {}, {}

        def take_bank(holder, shape):
            held_bank[holder] = free_banks.pop(0)
            return bank(held_bank[holder], shape, F32)

        def state(d, e):
            if d not in state_of:
                s_t = post.tile([P, VALS], F32, name="s_t")
                state_of[d] = s_t
            columns = slice(e * HALF, e * HALF + HALF)
            nc.vector.scalar_tensor_tensor(
                out=state_of[d][:, columns],
                in0=prev[:, d, columns],
                scalar=decay_cols[:, d : d + 1],
                in1=kv[d, e][:],
                op0=MULT,
                op1=ADD,
            )
            free_banks.append(2 * d + e)
            if e == HALVES - 1:
                nc.sync.dma_start(out=state_out[d * P : d * P + P, :], in_=state_of[d][:])

        def gained(d):
            h_t = post.tile([P, VALS], BF16, name="h_t", bufs=2)
            h_of[d] = h_t
            for e in range(HALVES):
                columns = slice(e * HALF, e * HALF + HALF)
                nc.vector.tensor_tensor(
                    out=h_t[:, columns], in0=state_of[d][:, columns], in1=gain_rows[:, columns], op=MULT
                )

        def turn(d):
            words = h_of[d][:].bitcast(F32)
            for g in range(2):
                x_t = take_bank(("turned", d, g), [P, 2, P])
                turned[d, g] = x_t
                for u in range(2):
                    nc.tensor.transpose(x_t[:, u, :], words[:, 256 * g + u : 256 * (g + 1) : 2], ident[:])
            for g in range(2):
                hg_t = post.tile([P, P, PACK], BF16, name="hg_t", align_bytes=64)
                h_grouped[d, g] = hg_t
                pairs = hg_t[:].rearrange("p r t -> p (r t)").bitcast(F32)
                nc.scalar.copy(
                    out=pairs.rearrange("p (r u) -> p r u", u=2), in_=turned[d, g][:].rearrange("p u r -> p r u")
                )
                free_banks.append(held_bank["turned", d, g])

        def quantise_h(d):
            for g in range(2):
                hc_t = post.tile([P, P], U32, name="hc_t", align_bytes=64)
                hp_t = post.tile([P, P], U8, name="hp_t", align_bytes=64)
                h_codes[d, g], h_planes[d, g] = hc_t, hp_t
                nc.vector.quantize_mx(
                    out=hc_t[:].bitcast(FP8X4), scales=hp_t[:], in_=h_grouped[d, g][:].rearrange("p r t -> p (r t)")
                )

        def project(d, n, engine_copy):
            if d not in y_of:
                y_t = post.tile([P, OUTS], F32, name="y_t", bufs=3)
                y_of[d] = y_t
            y_p = take_bank(("y", d, n), [P, HALF])
            columns = slice(n * HALF, n * HALF + HALF)
            for g in range(2):
                nc.tensor.matmul_mx(
                    out=y_p[:],
                    lhsT=h_codes[d, g][:].bitcast(FP8X4),
                    lhsT_scale=h_planes[d, g][:],
                    rhs=w_codes[:, g, 2 * n * HALF : 2 * (n + 1) * HALF].bitcast(FP4X4),
                    rhs_scale=w_scale_rows[:, g, columns],
                    start=(g == 0),
                    stop=(g == 1),
                )
            engine_copy(out=y_of[d][:, columns], in_=y_p[:])
            free_banks.append(held_bank["y", d, n])
            nc.sync.dma_start(out=y_out[d * P : d * P + P, columns], in_=y_of[d][:, columns])

        state(0, 0)
        state(1, 0)
        state(0, 1)
        gained(0)
        turn(0)
        state(1, 1)
        for d in range(KEY_TILES):
            quantise_h(d)
            for n in range(OUTS // HALF):
                if n == 2 and d + 1 < KEY_TILES:
                    gained(d + 1)
                    turn(d + 1)
                    if d + 2 < KEY_TILES:
                        state(d + 2, 0)
                        state(d + 2, 1)
                on_vector = d == KEY_TILES - 1 and n % 2 == 0
                project(d, n, nc.vector.tensor_copy if on_vector else nc.scalar.copy)
